import numpy as np
import ml_dtypes


def mxq(x, axis, fmt="e4m3"):
    dtype, down = {"e4m3": (ml_dtypes.float8_e4m3fn, 7), "e5m2": (ml_dtypes.float8_e5m2, 14)}[fmt]
    v = np.moveaxis(np.asarray(x, np.float32).astype(ml_dtypes.bfloat16).astype(np.float64), axis, -1)
    blocks = v.reshape(v.shape[:-1] + (-1, 32))
    amax = np.abs(blocks).max(-1, keepdims=True)
    byte = np.maximum(np.where(amax > 0, np.frexp(amax)[1] - 1 + 127, 0) - down, 1)
    scale = np.exp2(byte - 127.0)
    codes = (blocks / scale).astype(np.float32).astype(dtype).astype(np.float64)
    return np.moveaxis((codes * scale).reshape(v.shape), -1, axis)


WIDE = False


def mx_kscale(k):
    if not WIDE:
        return np.ones(k)
    levels = np.array([10, -10, 5, -5, 0])
    if k % 512:
        return np.exp2(np.random.permutation(np.resize(levels, k // 32))).repeat(32)
    a = np.empty((k // 512, 16))
    for p in range(k // 512):
        a[p, :8] = np.random.permutation(np.resize(levels, 8))
        for g in range(8):
            far = levels[np.abs(levels - a[p, g]) >= 10]
            a[p, g + 8] = far[np.random.randint(len(far))]
    return np.exp2(a.ravel()).repeat(32)


BF16 = ml_dtypes.bfloat16


def bf(x):
    return np.asarray(x, np.float32).astype(BF16)


def f64(x):
    return np.asarray(x).astype(np.float64)


E2M1 = np.array([0.0, 0.5, 1.0, 1.5, 2.0, 3.0, 4.0, 6.0, -0.0, -0.5, -1.0, -1.5, -2.0, -3.0, -4.0, -6.0])


def pack_weight(w, fmt):
    k, n = w.shape
    w = f64(bf(w)).reshape(k // 32, 32, n)
    amax = np.abs(w).max(1)
    if fmt == "e4m3":
        byte = np.frexp(amax)[1] - 1 + 127 - 7
    else:
        mant, ex = np.frexp(amax / 6.0)
        byte = np.where(mant > 0.5, ex, ex - 1) + 127
    byte = np.clip(np.where(amax > 0, byte, 1), 1, 254)
    scaled = (w * np.exp2(127.0 - byte)[:, None, :]).reshape(k, n).astype(np.float32)
    by_word = np.ascontiguousarray(scaled.reshape(k // 512, 128, 4, n).transpose(0, 1, 3, 2))
    if fmt == "e4m3":
        words = by_word.astype(ml_dtypes.float8_e4m3fn).view(np.uint8)
    else:
        c = by_word.astype(ml_dtypes.float4_e2m1fn).view(np.uint8) & 0xF
        words = c[..., 0::2] | (c[..., 1::2] << 4)
    return np.ascontiguousarray(words), np.ascontiguousarray(byte.astype(np.uint8).reshape(k // 512, 16, n))


def unpack_weight(words, scales, fmt):
    g, p, n, _ = words.shape
    if fmt == "e4m3":
        vals = np.ascontiguousarray(words).view(ml_dtypes.float8_e4m3fn).astype(np.float64)
    else:
        nib = np.empty((g, p, n, 4), np.uint8)
        nib[..., 0::2] = words & 0xF
        nib[..., 1::2] = words >> 4
        vals = E2M1[nib]
    vals = vals * np.repeat(np.exp2(scales.astype(np.float64) - 127.0), 8, axis=1)[..., None]
    return vals.transpose(0, 1, 3, 2).reshape(g * 512, n)
def pack4(w):
    words, scales = pack_weight(w, "e2m1")
    return words.reshape(words.shape[0], 128, -1), scales


def unpack4(words, scales):
    return unpack_weight(words.reshape(words.shape[0], 128, -1, 2), scales, "e2m1")


T, F, C, D, J = 2048, 1024, 1024, 1024, 512


def setup_inputs():
    s, r, v = mx_kscale(F), mx_kscale(D), mx_kscale(C)
    x = np.random.standard_normal((T, F)) * s
    mu = np.random.standard_normal((F, C)) / np.sqrt(F) / s[:, None]
    prior = np.exp(0.3 * np.random.standard_normal(C)) / np.sqrt(C) * v
    a = np.random.standard_normal((D, C)) / np.sqrt(D) * r[:, None] / v
    z = np.random.standard_normal((D, J)) / r[:, None]
    offset = 0.4 * np.random.standard_normal(C) / v
    a_words, a_scales = pack4(a)
    z_words, z_scales = pack4(z)
    return {"x": bf(x), "mu": bf(mu), "prior": bf(prior),
            "a_words": a_words, "a_scales": a_scales,
            "z_words": z_words, "z_scales": z_scales,
            "offset": bf(offset)}


def reference(x, mu, prior, a_words, a_scales, z_words, z_scales, offset):
    logits = mxq(f64(x), 1, "e4m3") @ mxq(f64(mu), 0, "e4m3")
    h = np.exp(logits) * f64(prior)
    local = (unpack4(a_words, a_scales).T @ unpack4(z_words, z_scales)) + f64(offset)[:, None]
    return mxq(h, 1, "e4m3") @ mxq(local, 0, "e4m3")

@@ -1,0 +1,360 @@
+from contextlib import ExitStack
+
+import concourse.mybir as mybir
+from concourse.masks import make_identity
+
+T, F, C, D, J = 2048, 1024, 1024, 1024, 512
+FLOPS = 2 * (T * F * C + D * C * J + T * C * J)
+
+F32 = mybir.dt.float32
+BF16 = mybir.dt.bfloat16
+I32 = mybir.dt.int32
+U32 = mybir.dt.uint32
+U8 = mybir.dt.uint8
+FP8X4 = mybir.dt.float8_e4m3fn_x4
+FP4X4 = mybir.dt.float4_e2m1fn_x4
+ACT = mybir.ActivationFunctionType
+ALU = mybir.AluOpType
+
+P = 128
+PACK = 4
+K_PASS = P * PACK
+PASSES = 2
+GROUP = 512
+HALF = GROUP // 2
+TILES_PER_GROUP = GROUP // P
+GROUPS = T // GROUP
+BANKS = 8
+RUN = 8
+LN_LOW = 2.0 ** -63
+LN_HIGH = 2.0 ** 63
+
+
+def tile_gaussian_mixture_skill_regression_s12_kernel(
+    tc, x, mu, prior, a_words, a_scales, z_words, z_scales, offset, out
+):
+    nc = tc.nc
+
+    with ExitStack() as ctx:
+        sb = ctx.enter_context(tc.tile_pool(name="sb", bufs=1))
+        psum = ctx.enter_context(tc.psum_pool(name="psum", bufs=1))
+        ctx.enter_context(tc.manual_schedule())
+
+        banks_taken = []
+
+        def next_bank(shape, dtype):
+            tag = "bank%d" % (len(banks_taken) % BANKS)
+            banks_taken.append(tag)
+            bank = psum.tile(shape, dtype, name=tag, tag=tag)
+            return bank
+
+        def quantize(grouped, width, tag, bufs):
+            codes = sb.tile([P, width], U32, name=tag + "_codes", tag=tag + "_codes", bufs=bufs, align_bytes=64)
+            scales = sb.tile([P, width], U8, name=tag + "_scales", tag=tag + "_scales", bufs=bufs, align_bytes=64)
+            nc.vector.quantize_mx(out=codes[:].bitcast(FP8X4), scales=scales[:], in_=grouped)
+            return codes, scales
+
+        def interleave(slots, width, tag, bufs):
+            grouped = sb.tile([P, width, PACK], BF16, name=tag, tag=tag, bufs=bufs, align_bytes=64)
+            nc.vector.tensor_copy(
+                out=grouped[:].rearrange("p (c i) t -> p c t i", i=4),
+                in_=slots.rearrange("p t (c i) -> p c t i", i=4),
+            )
+            return grouped[:].rearrange("p n t -> p (n t)")
+
+        a_scale_raw = sb.tile([P, PASSES, C], U8, align_bytes=64)
+        z_scale = sb.tile([P, PASSES, J], U8, align_bytes=64)
+        vec_rows = sb.tile([P, 2 * P], BF16)
+        one = sb.tile([P, 1], F32)
+        nc.vector.memset(vec_rows[:], 0.0)
+        nc.vector.memset(a_scale_raw[:].bitcast(I32), 0)
+        nc.vector.memset(z_scale[:].bitcast(I32), 0)
+        nc.vector.memset(one[:], 1.0)
+
+        table_out = sb.tile([P, 2], F32)
+        nc.scalar.activation(out=table_out[:, 0:1], in_=one[:], func=ACT.Ln)
+
+        ident_bf = sb.tile([P, P], BF16)
+        ident_f32 = sb.tile([P, P], F32)
+        make_identity(nc, ident_bf[:])
+        make_identity(nc, ident_f32[:])
+
+        a_raw = sb.tile([P, PASSES, 2 * C], U8, align_bytes=64)
+        z_codes = sb.tile([P, PASSES, 2 * J], U8, align_bytes=64)
+
+        def load_scales(plane, rows):
+            for quad in range(4):
+                nc.sync.dma_start(
+                    out=plane[32 * quad : 32 * quad + 4, :, :].bitcast(I32),
+                    in_=rows[:, 4 * quad : 4 * quad + 4, :].rearrange("g r n -> r g n").bitcast(I32),
+                )
+
+        mu_raw = {}
+        x_rows = {}
+
+        def load_mu(kp, cp):
+            raw = sb.tile([P, PACK, K_PASS], BF16, name="mu_raw", tag="mu_raw", bufs=4)
+            nc.sync.dma_start(
+                out=raw[:],
+                in_=mu[kp * K_PASS : (kp + 1) * K_PASS, cp * K_PASS : (cp + 1) * K_PASS].rearrange(
+                    "(p j) c -> p j c", j=PACK
+                ),
+            )
+            mu_raw[kp, cp] = raw
+
+        def load_x(first, count):
+            tag = "x_rows%d" % first
+            rows = sb.tile([P, count, F], BF16, name=tag, tag=tag)
+            nc.sync.dma_start(
+                out=rows[:], in_=x[first * P : (first + count) * P, :].rearrange("(a p) k -> p a k", p=P)
+            )
+            for i in range(count):
+                x_rows[first + i] = rows[:, i, :]
+
+        for row0, vec in ((0, prior), (PACK, offset)):
+            nc.sync.dma_start(
+                out=vec_rows[row0 : row0 + PACK, :].rearrange("t (b r) -> t b r", r=RUN),
+                in_=vec.rearrange("(b t r) -> t b r", t=PACK, r=RUN),
+            )
+        load_x(0, 2)
+        load_scales(a_scale_raw, a_scales)
+        nc.sync.dma_start(out=a_raw[:].bitcast(I32), in_=a_words.rearrange("g p n -> p g n").bitcast(I32))
+        nc.sync.dma_start(out=z_codes[:].bitcast(I32), in_=z_words.rearrange("g p n -> p g n").bitcast(I32))
+        load_scales(z_scale, z_scales)
+        load_mu(0, 0)
+        load_mu(1, 0)
+        load_x(2, 2)
+        load_mu(0, 1)
+        load_mu(1, 1)
+        for a in range(4, T // P, 2):
+            load_x(a, 2)
+
+        vec_bank = next_bank([P, PASSES, P], BF16)
+        for cp in range(PASSES):
+            nc.tensor.transpose(vec_bank[:, cp, :], vec_rows[:, cp * P : (cp + 1) * P], ident_bf[:])
+        vecs = sb.tile([P, PASSES, 2 * PACK], F32)
+        nc.vector.tensor_copy(out=vecs[:], in_=vec_bank[:, :, 0 : 2 * PACK])
+        pri = vecs[:, :, 0:PACK]
+        off = vecs[:, :, PACK : 2 * PACK]
+        sign01 = sb.tile([P, PASSES, PACK], F32)
+        sign = sb.tile([P, PASSES, PACK], F32)
+        mag = sb.tile([P, PASSES, PACK], F32)
+        below = sb.tile([P, PASSES, PACK], F32)
+        above = sb.tile([P, PASSES, PACK], F32)
+        factors = sb.tile([P, 2, PASSES, PACK], F32)
+        signed_off = sb.tile([P, PASSES, PACK], F32)
+        nc.vector.tensor_scalar(out=sign01[:], in0=pri, scalar1=0.0, scalar2=2.0, op0=ALU.is_ge, op1=ALU.mult)
+        nc.vector.scalar_tensor_tensor(out=mag[:], in0=pri, scalar=-1.0, in1=pri, op0=ALU.mult, op1=ALU.max)
+        nc.vector.tensor_scalar(out=sign[:], in0=sign01[:], scalar1=-1.0, scalar2=None, op0=ALU.add)
+        nc.vector.tensor_scalar(out=below[:], in0=mag[:], scalar1=LN_LOW, scalar2=LN_HIGH, op0=ALU.min, op1=ALU.mult)
+        nc.vector.tensor_scalar(out=above[:], in0=mag[:], scalar1=LN_HIGH, scalar2=LN_LOW, op0=ALU.max, op1=ALU.mult)
+        nc.vector.tensor_scalar(out=factors[:, 0], in0=mag[:], scalar1=LN_LOW, scalar2=LN_HIGH, op0=ALU.max, op1=ALU.min)
+        nc.vector.tensor_tensor(out=signed_off[:], in0=off, in1=sign[:], op=ALU.mult)
+        nc.vector.scalar_tensor_tensor(
+            out=factors[:, 1], in0=below[:], scalar=LN_LOW, in1=above[:], op0=ALU.max, op1=ALU.mult
+        )
+        logs = sb.tile([P, 2, PASSES, PACK], F32)
+        log_prior = sb.tile([P, PASSES, PACK], F32)
+
+        a_codes = sb.tile([P, PASSES, 2 * C], U8, align_bytes=64)
+        a_scale = sb.tile([P, PASSES, C], U8, align_bytes=64)
+        for dst, src, words in ((a_scale, a_scale_raw, 2), (a_codes, a_raw, 4)):
+            nc.vector.tensor_copy(
+                out=dst[:].bitcast(I32).rearrange("p g (h t q w) -> p (g h) t q w", h=PASSES, t=PACK, w=words),
+                in_=src[:].bitcast(I32).rearrange("p g (h q t w) -> p (g h) t q w", h=PASSES, t=PACK, w=words),
+            )
+
+        mu_grouped = {}
+        mu_q = {}
+        l_slots = {}
+        l_grouped = {}
+        l_q = {}
+        x_grouped = {}
+        x_q = {}
+        h_slots = {}
+        h_q = {}
+        out_banks = {}
+
+        def interleave_mu(kp, cp):
+            grouped = sb.tile([P, PACK, P, PACK], BF16, name="mu_grouped", tag="mu_grouped", bufs=2, align_bytes=64)
+            src = mu_raw[kp, cp][:].rearrange("p j (q t h i) -> p t q h j i", t=PACK, h=2, i=4)
+            dst = grouped[:].rearrange("p t (q h i) j -> p t q h j i", h=2, i=4)
+            for t in range(PACK):
+                nc.vector.tensor_copy(out=dst[:, t], in_=src[:, t])
+            mu_grouped[kp, cp] = grouped[:].rearrange("p t m j -> p (t m j)")
+
+        def quantize_mu(kp, cp):
+            mu_q[kp, cp] = quantize(mu_grouped[kp, cp], K_PASS, "mu", 4)
+
+        def local_models(cp, t):
+            if t == 0:
+                l_slots[cp] = sb.tile([P, PACK, J], BF16, name="l_slots", tag="l_slots", bufs=2)
+            bank = next_bank([P, J], F32)
+            col = (cp * PACK + t) * P
+            for kp in range(PASSES):
+                nc.tensor.matmul_mx(
+                    out=bank[:],
+                    lhsT=a_codes[:, kp, 2 * col : 2 * (col + P)].bitcast(FP4X4),
+                    lhsT_scale=a_scale[:, kp, col : col + P],
+                    rhs=z_codes[:, kp, :].bitcast(FP4X4),
+                    rhs_scale=z_scale[:, kp, :],
+                    start=(kp == 0),
+                    stop=(kp == PASSES - 1),
+                )
+            nc.scalar.activation(
+                out=l_slots[cp][:, t, :],
+                in_=bank[:],
+                func=ACT.Identity,
+                scale=sign[:, cp, t : t + 1],
+                bias=signed_off[:, cp, t : t + 1],
+            )
+
+        def interleave_l(cp):
+            l_grouped[cp] = interleave(l_slots[cp][:], J, "l_grouped", 2)
+
+        def quantize_l(cp):
+            l_q[cp] = quantize(l_grouped[cp], J, "l", 2)
+
+        def turn_x(tiles):
+            turned = []
+            for a in tiles:
+                bank = next_bank([P, PASSES, 2, P], F32)
+                words = x_rows[a].bitcast(F32)
+                for kp in range(PASSES):
+                    for u in range(2):
+                        nc.tensor.transpose(
+                            bank[:, kp, u, :], words[:, 256 * kp + u : 256 * (kp + 1) : 2], ident_f32[:]
+                        )
+                turned.append((a, bank))
+            for a, bank in turned:
+                g, i = divmod(a, TILES_PER_GROUP)
+                if i == 0:
+                    x_grouped[g] = sb.tile(
+                        [P, PASSES, GROUP, 2], F32, name="x_grouped", tag="x_grouped", bufs=2, align_bytes=64
+                    )
+                nc.scalar.copy(
+                    out=x_grouped[g][:, :, i * P : (i + 1) * P, :], in_=bank[:].rearrange("p g u r -> p g r u")
+                )
+
+        def quantize_x(g):
+            for kp in range(PASSES):
+                grouped = x_grouped[g][:, kp].rearrange("p n u -> p (n u)").bitcast(BF16)
+                x_q[g, kp] = quantize(grouped, GROUP, "x", 4)
+
+        def responsibilities(g, cp):
+            slots = sb.tile([P, PACK, GROUP], BF16, name="h_slots", tag="h_slots", bufs=3)
+            for t in range(PACK):
+                bank = next_bank([P, GROUP], F32)
+                for kp in range(PASSES):
+                    w_codes, w_scales = mu_q[kp, cp]
+                    x_codes, x_scales = x_q[g, kp]
+                    nc.tensor.matmul_mx(
+                        out=bank[:],
+                        lhsT=w_codes[:, t * P : (t + 1) * P].bitcast(FP8X4),
+                        lhsT_scale=w_scales[:, t * P : (t + 1) * P],
+                        rhs=x_codes[:].bitcast(FP8X4),
+                        rhs_scale=x_scales[:],
+                        start=(kp == 0),
+                        stop=(kp == PASSES - 1),
+                    )
+                nc.scalar.activation(
+                    out=slots[:, t, :], in_=bank[:], func=ACT.Exp, bias=log_prior[:, cp, t : t + 1]
+                )
+            h_slots[g, cp] = slots
+
+        def quantize_h(g, cp):
+            halves = []
+            for half in range(2):
+                halves.append(interleave(h_slots[g, cp][:, :, half * HALF : (half + 1) * HALF], HALF, "h_grouped", 4))
+            for half in range(2):
+                h_q[g, cp, half] = quantize(halves[half], HALF, "h", 10)
+
+        def blend(a):
+            g, i = divmod(a, TILES_PER_GROUP)
+            half, j = divmod(i, 2)
+            bank = next_bank([P, J], F32)
+            for cp in range(PASSES):
+                h_codes, h_scales = h_q[g, cp, half]
+                l_codes, l_scales = l_q[cp]
+                nc.tensor.matmul_mx(
+                    out=bank[:],
+                    lhsT=h_codes[:, j * P : (j + 1) * P].bitcast(FP8X4),
+                    lhsT_scale=h_scales[:, j * P : (j + 1) * P],
+                    rhs=l_codes[:].bitcast(FP8X4),
+                    rhs_scale=l_scales[:],
+                    start=(cp == 0),
+                    stop=(cp == PASSES - 1),
+                )
+            out_banks[a] = bank
+
+        def store(a, on_scalar):
+            result = sb.tile([P, J], F32, name="result", tag="result", bufs=6)
+            if on_scalar:
+                nc.scalar.copy(out=result[:], in_=out_banks[a][:])
+            else:
+                nc.vector.tensor_copy(out=result[:], in_=out_banks[a][:])
+            nc.sync.dma_start(out=out[a * P : (a + 1) * P, :], in_=result[:])
+
+        turn_x((0, 1))
+        nc.scalar.activation(out=logs[:], in_=factors[:], func=ACT.Ln)
+        nc.scalar.activation(out=table_out[:, 1:2], in_=one[:], func=ACT.Exp)
+        interleave_mu(0, 0)
+        interleave_mu(1, 0)
+        nc.vector.tensor_tensor(out=log_prior[:], in0=logs[:, 0], in1=logs[:, 1], op=ALU.add)
+        quantize_mu(0, 0)
+        quantize_mu(1, 0)
+        for t in range(PACK):
+            local_models(0, t)
+        local_models(1, 0)
+        turn_x((2, 3))
+        for t in range(1, PACK):
+            local_models(1, t)
+        quantize_x(0)
+        interleave_mu(0, 1)
+        interleave_mu(1, 1)
+        quantize_mu(0, 1)
+        quantize_mu(1, 1)
+
+        responsibilities(0, 0)
+        turn_x((4, 5, 6, 7))
+        interleave_l(0)
+        interleave_l(1)
+        quantize_x(1)
+        quantize_l(0)
+        quantize_l(1)
+        responsibilities(0, 1)
+        quantize_h(0, 0)
+        turn_x((8, 9))
+
+        for g in (1, 2):
+            done = TILES_PER_GROUP * (g - 1)
+            ahead = TILES_PER_GROUP * (g + 1)
+            responsibilities(g, 0)
+            quantize_h(g - 1, 1)
+            turn_x((ahead + 2, ahead + 3))
+            blend(done)
+            blend(done + 1)
+            store(done, True)
+            quantize_h(g, 0)
+            store(done + 1, False)
+            responsibilities(g, 1)
+            quantize_x(g + 1)
+            if g + 2 < GROUPS:
+                turn_x((ahead + 4, ahead + 5))
+            blend(done + 2)
+            blend(done + 3)
+            store(done + 2, True)
+            store(done + 3, False)
+
+        g = GROUPS - 1
+        responsibilities(g, 0)
+        quantize_h(g - 1, 1)
+        responsibilities(g, 1)
+        quantize_h(g, 0)
+        quantize_h(g, 1)
+        for a in range(TILES_PER_GROUP * (g - 1), TILES_PER_GROUP * g):
+            blend(a)
+            store(a, True)
+        for a in range(TILES_PER_GROUP * g, T // P):
+            blend(a)
+            store(a, a % 2 == 0)

@@ -66,8 +66,8 @@ def tile_gaussian_mixture_skill_regression_s12_kernel(
         z_scale = sb.tile([P, PASSES, J], U8, align_bytes=64)
         vec_rows = sb.tile([P, 2 * P], BF16)
         one = sb.tile([P, 1], F32)
-        nc.vector.memset(vec_rows[:], 0.0)
-        nc.vector.memset(a_scale_raw[:].bitcast(I32), 0)
+        nc.gpsimd.memset(vec_rows[:].bitcast(I32), 0)
+        nc.gpsimd.memset(a_scale_raw[:].bitcast(I32), 0)
         nc.vector.memset(z_scale[:].bitcast(I32), 0)
         nc.vector.memset(one[:], 1.0)
 
@@ -79,8 +79,13 @@ def tile_gaussian_mixture_skill_regression_s12_kernel(
         make_identity(nc, ident_bf[:])
         make_identity(nc, ident_f32[:])
 
-        a_raw = sb.tile([P, PASSES, 2 * C], U8, align_bytes=64)
+        a_raw = {}
         z_codes = sb.tile([P, PASSES, 2 * J], U8, align_bytes=64)
+
+        def load_a(cp):
+            a_raw[cp] = sb.tile([P, PASSES, 2 * K_PASS], U8, name="a_raw", tag="a_raw", bufs=2)
+            columns = a_words[:, :, 2 * K_PASS * cp : 2 * K_PASS * (cp + 1)]
+            nc.sync.dma_start(out=a_raw[cp][:].bitcast(I32), in_=columns.rearrange("g p n -> p g n").bitcast(I32))
 
         def load_scales(plane, rows):
             for quad in range(4):
@@ -91,6 +96,8 @@ def tile_gaussian_mixture_skill_regression_s12_kernel(
 
         mu_raw = {}
         x_rows = {}
+        x_pairs = {}
+        x_sorted = {}
 
         def load_mu(kp, cp):
             raw = sb.tile([P, PACK, K_PASS], BF16, name="mu_raw", tag="mu_raw", bufs=4)
@@ -108,6 +115,7 @@ def tile_gaussian_mixture_skill_regression_s12_kernel(
             nc.sync.dma_start(
                 out=rows[:], in_=x[first * P : (first + count) * P, :].rearrange("(a p) k -> p a k", p=P)
             )
+            x_pairs[first] = rows
             for i in range(count):
                 x_rows[first + i] = rows[:, i, :]
 
@@ -116,24 +124,21 @@ def tile_gaussian_mixture_skill_regression_s12_kernel(
                 out=vec_rows[row0 : row0 + PACK, :].rearrange("t (b r) -> t b r", r=RUN),
                 in_=vec.rearrange("(b t r) -> t b r", t=PACK, r=RUN),
             )
-        load_x(0, 2)
         load_scales(a_scale_raw, a_scales)
-        nc.sync.dma_start(out=a_raw[:].bitcast(I32), in_=a_words.rearrange("g p n -> p g n").bitcast(I32))
+        load_a(0)
         nc.sync.dma_start(out=z_codes[:].bitcast(I32), in_=z_words.rearrange("g p n -> p g n").bitcast(I32))
         load_scales(z_scale, z_scales)
+        load_a(1)
         load_mu(0, 0)
-        load_mu(1, 0)
+        load_x(0, 2)
         load_x(2, 2)
+        load_mu(1, 0)
         load_mu(0, 1)
         load_mu(1, 1)
         for a in range(4, T // P, 2):
             load_x(a, 2)
 
-        vec_bank = next_bank([P, PASSES, P], BF16)
-        for cp in range(PASSES):
-            nc.tensor.transpose(vec_bank[:, cp, :], vec_rows[:, cp * P : (cp + 1) * P], ident_bf[:])
         vecs = sb.tile([P, PASSES, 2 * PACK], F32)
-        nc.vector.tensor_copy(out=vecs[:], in_=vec_bank[:, :, 0 : 2 * PACK])
         pri = vecs[:, :, 0:PACK]
         off = vecs[:, :, PACK : 2 * PACK]
         sign01 = sb.tile([P, PASSES, PACK], F32)
@@ -143,25 +148,40 @@ def tile_gaussian_mixture_skill_regression_s12_kernel(
         above = sb.tile([P, PASSES, PACK], F32)
         factors = sb.tile([P, 2, PASSES, PACK], F32)
         signed_off = sb.tile([P, PASSES, PACK], F32)
-        nc.vector.tensor_scalar(out=sign01[:], in0=pri, scalar1=0.0, scalar2=2.0, op0=ALU.is_ge, op1=ALU.mult)
-        nc.vector.scalar_tensor_tensor(out=mag[:], in0=pri, scalar=-1.0, in1=pri, op0=ALU.mult, op1=ALU.max)
-        nc.vector.tensor_scalar(out=sign[:], in0=sign01[:], scalar1=-1.0, scalar2=None, op0=ALU.add)
-        nc.vector.tensor_scalar(out=below[:], in0=mag[:], scalar1=LN_LOW, scalar2=LN_HIGH, op0=ALU.min, op1=ALU.mult)
-        nc.vector.tensor_scalar(out=above[:], in0=mag[:], scalar1=LN_HIGH, scalar2=LN_LOW, op0=ALU.max, op1=ALU.mult)
-        nc.vector.tensor_scalar(out=factors[:, 0], in0=mag[:], scalar1=LN_LOW, scalar2=LN_HIGH, op0=ALU.max, op1=ALU.min)
-        nc.vector.tensor_tensor(out=signed_off[:], in0=off, in1=sign[:], op=ALU.mult)
-        nc.vector.scalar_tensor_tensor(
-            out=factors[:, 1], in0=below[:], scalar=LN_LOW, in1=above[:], op0=ALU.max, op1=ALU.mult
-        )
+
+        def spread_vectors():
+            vec_bank = next_bank([P, PASSES, P], BF16)
+            for cp in range(PASSES):
+                nc.tensor.transpose(vec_bank[:, cp, :], vec_rows[:, cp * P : (cp + 1) * P], ident_bf[:])
+            nc.vector.tensor_copy(out=vecs[:], in_=vec_bank[:, :, 0 : 2 * PACK])
+            nc.vector.tensor_scalar(out=sign01[:], in0=pri, scalar1=0.0, scalar2=2.0, op0=ALU.is_ge, op1=ALU.mult)
+            nc.vector.scalar_tensor_tensor(out=mag[:], in0=pri, scalar=-1.0, in1=pri, op0=ALU.mult, op1=ALU.max)
+            nc.vector.tensor_scalar(out=sign[:], in0=sign01[:], scalar1=-1.0, scalar2=None, op0=ALU.add)
+            nc.vector.tensor_scalar(out=below[:], in0=mag[:], scalar1=LN_LOW, scalar2=LN_HIGH, op0=ALU.min, op1=ALU.mult)
+            nc.vector.tensor_scalar(out=above[:], in0=mag[:], scalar1=LN_HIGH, scalar2=LN_LOW, op0=ALU.max, op1=ALU.mult)
+            nc.vector.tensor_scalar(out=factors[:, 0], in0=mag[:], scalar1=LN_LOW, scalar2=LN_HIGH, op0=ALU.max, op1=ALU.min)
+            nc.vector.tensor_tensor(out=signed_off[:], in0=off, in1=sign[:], op=ALU.mult)
+            nc.vector.scalar_tensor_tensor(
+                out=factors[:, 1], in0=below[:], scalar=LN_LOW, in1=above[:], op0=ALU.max, op1=ALU.mult
+            )
+
         logs = sb.tile([P, 2, PASSES, PACK], F32)
         log_prior = sb.tile([P, PASSES, PACK], F32)
 
-        a_codes = sb.tile([P, PASSES, 2 * C], U8, align_bytes=64)
         a_scale = sb.tile([P, PASSES, C], U8, align_bytes=64)
-        for dst, src, words in ((a_scale, a_scale_raw, 2), (a_codes, a_raw, 4)):
+        a_codes = {}
+
+        def sort_a_scales():
             nc.vector.tensor_copy(
-                out=dst[:].bitcast(I32).rearrange("p g (h t q w) -> p (g h) t q w", h=PASSES, t=PACK, w=words),
-                in_=src[:].bitcast(I32).rearrange("p g (h q t w) -> p (g h) t q w", h=PASSES, t=PACK, w=words),
+                out=a_scale[:].bitcast(I32).rearrange("p g (h t q w) -> p (g h) t q w", h=PASSES, t=PACK, w=2),
+                in_=a_scale_raw[:].bitcast(I32).rearrange("p g (h q t w) -> p (g h) t q w", h=PASSES, t=PACK, w=2),
+            )
+
+        def sort_a(cp):
+            a_codes[cp] = sb.tile([P, PASSES, 2 * K_PASS], U8, name="a_codes", tag="a_codes", bufs=2, align_bytes=64)
+            nc.vector.tensor_copy(
+                out=a_codes[cp][:].bitcast(I32).rearrange("p g (t q w) -> p g t q w", t=PACK, w=4),
+                in_=a_raw[cp][:].bitcast(I32).rearrange("p g (q t w) -> p g t q w", t=PACK, w=4),
             )
 
         mu_grouped = {}
@@ -194,7 +214,7 @@ def tile_gaussian_mixture_skill_regression_s12_kernel(
             for kp in range(PASSES):
                 nc.tensor.matmul_mx(
                     out=bank[:],
-                    lhsT=a_codes[:, kp, 2 * col : 2 * (col + P)].bitcast(FP4X4),
+                    lhsT=a_codes[cp][:, kp, 2 * t * P : 2 * (t + 1) * P].bitcast(FP4X4),
                     lhsT_scale=a_scale[:, kp, col : col + P],
                     rhs=z_codes[:, kp, :].bitcast(FP4X4),
                     rhs_scale=z_scale[:, kp, :],
@@ -215,16 +235,27 @@ def tile_gaussian_mixture_skill_regression_s12_kernel(
         def quantize_l(cp):
             l_q[cp] = quantize(l_grouped[cp], J, "l", 2)
 
-        def turn_x(tiles):
+        def sort_x(first):
+            ordered = sb.tile([P, 2, PASSES, 2, P], F32, name="x_sorted", tag="x_sorted", bufs=2)
+            nc.vector.tensor_copy(
+                out=ordered[:].rearrange("p a g u (c i) -> p (a g) c u i", i=4),
+                in_=x_pairs[first][:].bitcast(F32).rearrange("p a (g c i u) -> p (a g) c u i", g=PASSES, i=4, u=2),
+            )
+            for i in range(2):
+                x_sorted[first + i] = ordered[:, i]
+
+        def turn_x(tiles, on_vector=()):
             turned = []
             for a in tiles:
                 bank = next_bank([P, PASSES, 2, P], F32)
                 words = x_rows[a].bitcast(F32)
                 for kp in range(PASSES):
                     for u in range(2):
-                        nc.tensor.transpose(
-                            bank[:, kp, u, :], words[:, 256 * kp + u : 256 * (kp + 1) : 2], ident_f32[:]
-                        )
+                        if a in x_sorted:
+                            source = x_sorted[a][:, kp, u, :]
+                        else:
+                            source = words[:, 256 * kp + u : 256 * (kp + 1) : 2]
+                        nc.tensor.transpose(bank[:, kp, u, :], source, ident_f32[:])
                 turned.append((a, bank))
             for a, bank in turned:
                 g, i = divmod(a, TILES_PER_GROUP)
@@ -232,19 +263,20 @@ def tile_gaussian_mixture_skill_regression_s12_kernel(
                     x_grouped[g] = sb.tile(
                         [P, PASSES, GROUP, 2], F32, name="x_grouped", tag="x_grouped", bufs=2, align_bytes=64
                     )
-                nc.scalar.copy(
-                    out=x_grouped[g][:, :, i * P : (i + 1) * P, :], in_=bank[:].rearrange("p g u r -> p g r u")
-                )
+                move = nc.vector.tensor_copy if a in on_vector else nc.scalar.copy
+                move(out=x_grouped[g][:, :, i * P : (i + 1) * P, :], in_=bank[:].rearrange("p g u r -> p g r u"))
 
         def quantize_x(g):
             for kp in range(PASSES):
                 grouped = x_grouped[g][:, kp].rearrange("p n u -> p (n u)").bitcast(BF16)
                 x_q[g, kp] = quantize(grouped, GROUP, "x", 4)
 
-        def responsibilities(g, cp):
-            slots = sb.tile([P, PACK, GROUP], BF16, name="h_slots", tag="h_slots", bufs=3)
+        def responsibilities(g, cp, col0=0, width=GROUP):
+            if col0 == 0:
+                h_slots[g, cp] = sb.tile([P, PACK, GROUP], BF16, name="h_slots", tag="h_slots", bufs=5)
+            cols = slice(col0, col0 + width)
             for t in range(PACK):
-                bank = next_bank([P, GROUP], F32)
+                bank = next_bank([P, width], F32)
                 for kp in range(PASSES):
                     w_codes, w_scales = mu_q[kp, cp]
                     x_codes, x_scales = x_q[g, kp]
@@ -252,62 +284,67 @@ def tile_gaussian_mixture_skill_regression_s12_kernel(
                         out=bank[:],
                         lhsT=w_codes[:, t * P : (t + 1) * P].bitcast(FP8X4),
                         lhsT_scale=w_scales[:, t * P : (t + 1) * P],
-                        rhs=x_codes[:].bitcast(FP8X4),
-                        rhs_scale=x_scales[:],
+                        rhs=x_codes[:, cols].bitcast(FP8X4),
+                        rhs_scale=x_scales[:, cols],
                         start=(kp == 0),
                         stop=(kp == PASSES - 1),
                     )
                 nc.scalar.activation(
-                    out=slots[:, t, :], in_=bank[:], func=ACT.Exp, bias=log_prior[:, cp, t : t + 1]
+                    out=h_slots[g, cp][:, t, cols], in_=bank[:], func=ACT.Exp, bias=log_prior[:, cp, t : t + 1]
                 )
-            h_slots[g, cp] = slots
 
-        def quantize_h(g, cp):
-            halves = []
-            for half in range(2):
-                halves.append(interleave(h_slots[g, cp][:, :, half * HALF : (half + 1) * HALF], HALF, "h_grouped", 4))
-            for half in range(2):
-                h_q[g, cp, half] = quantize(halves[half], HALF, "h", 10)
+        def quantize_h(g, cp, width, col0=0, count=2):
+            tag = "h%d" % width
+            grouped = []
+            for i in range(count + 1):
+                if i < count:
+                    slots = h_slots[g, cp][:, :, col0 + i * width : col0 + (i + 1) * width]
+                    grouped.append(interleave(slots, width, tag + "_grouped", 4))
+                if i > 0:
+                    codes, scales = quantize(grouped[i - 1], width, tag, 10)
+                    first = g * TILES_PER_GROUP + (col0 + (i - 1) * width) // P
+                    for j in range(width // P):
+                        h_q[first + j, cp] = (codes[:, j * P : (j + 1) * P], scales[:, j * P : (j + 1) * P])
 
-        def blend(a):
-            g, i = divmod(a, TILES_PER_GROUP)
-            half, j = divmod(i, 2)
-            bank = next_bank([P, J], F32)
+        def blend(a, col0=0, width=J):
+            bank = next_bank([P, width], F32)
             for cp in range(PASSES):
-                h_codes, h_scales = h_q[g, cp, half]
+                h_codes, h_scales = h_q[a, cp]
                 l_codes, l_scales = l_q[cp]
                 nc.tensor.matmul_mx(
                     out=bank[:],
-                    lhsT=h_codes[:, j * P : (j + 1) * P].bitcast(FP8X4),
-                    lhsT_scale=h_scales[:, j * P : (j + 1) * P],
-                    rhs=l_codes[:].bitcast(FP8X4),
-                    rhs_scale=l_scales[:],
+                    lhsT=h_codes.bitcast(FP8X4),
+                    lhsT_scale=h_scales,
+                    rhs=l_codes[:, col0 : col0 + width].bitcast(FP8X4),
+                    rhs_scale=l_scales[:, col0 : col0 + width],
                     start=(cp == 0),
                     stop=(cp == PASSES - 1),
                 )
-            out_banks[a] = bank
+            out_banks[a, col0] = bank
 
-        def store(a, on_scalar):
-            result = sb.tile([P, J], F32, name="result", tag="result", bufs=6)
+        def store(a, on_scalar, col0=0, width=J):
+            result = sb.tile([P, width], F32, name="result", tag="result", bufs=8)
             if on_scalar:
-                nc.scalar.copy(out=result[:], in_=out_banks[a][:])
+                nc.scalar.copy(out=result[:], in_=out_banks[a, col0][:])
             else:
-                nc.vector.tensor_copy(out=result[:], in_=out_banks[a][:])
-            nc.sync.dma_start(out=out[a * P : (a + 1) * P, :], in_=result[:])
+                nc.vector.tensor_copy(out=result[:], in_=out_banks[a, col0][:])
+            nc.sync.dma_start(out=out[a * P : (a + 1) * P, col0 : col0 + width], in_=result[:])
 
-        turn_x((0, 1))
+        spread_vectors()
+        sort_a_scales()
+        sort_a(0)
+        sort_a(1)
         nc.scalar.activation(out=logs[:], in_=factors[:], func=ACT.Ln)
         nc.scalar.activation(out=table_out[:, 1:2], in_=one[:], func=ACT.Exp)
         interleave_mu(0, 0)
-        interleave_mu(1, 0)
         nc.vector.tensor_tensor(out=log_prior[:], in0=logs[:, 0], in1=logs[:, 1], op=ALU.add)
         quantize_mu(0, 0)
-        quantize_mu(1, 0)
         for t in range(PACK):
             local_models(0, t)
-        local_models(1, 0)
-        turn_x((2, 3))
-        for t in range(1, PACK):
+        turn_x(range(0, 4))
+        interleave_mu(1, 0)
+        quantize_mu(1, 0)
+        for t in range(PACK):
             local_models(1, t)
         quantize_x(0)
         interleave_mu(0, 1)
@@ -316,45 +353,51 @@ def tile_gaussian_mixture_skill_regression_s12_kernel(
         quantize_mu(1, 1)
 
         responsibilities(0, 0)
-        turn_x((4, 5, 6, 7))
         interleave_l(0)
-        interleave_l(1)
+        turn_x(range(4, 8), ())
         quantize_x(1)
+        responsibilities(0, 1)
+
+        responsibilities(1, 0)
+        interleave_l(1)
         quantize_l(0)
         quantize_l(1)
-        responsibilities(0, 1)
-        quantize_h(0, 0)
-        turn_x((8, 9))
 
-        for g in (1, 2):
-            done = TILES_PER_GROUP * (g - 1)
-            ahead = TILES_PER_GROUP * (g + 1)
-            responsibilities(g, 0)
-            quantize_h(g - 1, 1)
-            turn_x((ahead + 2, ahead + 3))
-            blend(done)
-            blend(done + 1)
-            store(done, True)
-            quantize_h(g, 0)
-            store(done + 1, False)
-            responsibilities(g, 1)
-            quantize_x(g + 1)
-            if g + 2 < GROUPS:
-                turn_x((ahead + 4, ahead + 5))
-            blend(done + 2)
-            blend(done + 3)
-            store(done + 2, True)
-            store(done + 3, False)
+        turn_x(range(8, 12), ())
+        quantize_h(0, 0, HALF)
+        quantize_h(0, 1, HALF)
+        responsibilities(1, 1)
+        quantize_x(2)
+        for a in range(0, 4):
+            blend(a)
+            store(a, a not in (7, 13))
 
-        g = GROUPS - 1
-        responsibilities(g, 0)
-        quantize_h(g - 1, 1)
-        responsibilities(g, 1)
-        quantize_h(g, 0)
-        quantize_h(g, 1)
-        for a in range(TILES_PER_GROUP * (g - 1), TILES_PER_GROUP * g):
+        sort_x(12)
+        sort_x(14)
+        responsibilities(2, 0)
+        quantize_h(1, 0, HALF)
+        quantize_h(1, 1, HALF)
+        turn_x(range(12, 16), (14, 15))
+        responsibilities(2, 1)
+        quantize_x(3)
+        quantize_h(2, 0, HALF)
+        for a in range(4, 8):
             blend(a)
-            store(a, True)
-        for a in range(TILES_PER_GROUP * g, T // P):
+        for a in range(4, 8):
+            if a not in (7, 13):
+                store(a, True)
+        quantize_h(2, 1, HALF)
+        for a in range(4, 8):
+            if a in (7, 13):
+                store(a, False)
+
+        responsibilities(3, 0)
+        quantize_h(3, 0, HALF)
+        responsibilities(3, 1)
+        quantize_h(3, 1, P, 0, 4)
+        for a in range(8, 15):
             blend(a)
-            store(a, a % 2 == 0)
+            store(a, a not in (7, 13))
+        for half in range(2):
+            blend(15, half * HALF, HALF)
+            store(15, half == 1, half * HALF, HALF)

@@ -66,18 +66,10 @@ def tile_gaussian_mixture_skill_regression_s12_kernel(
         z_scale = sb.tile([P, PASSES, J], U8, align_bytes=64)
         vec_rows = sb.tile([P, 2 * P], BF16)
         one = sb.tile([P, 1], F32)
-        nc.gpsimd.memset(vec_rows[:].bitcast(I32), 0)
-        nc.gpsimd.memset(a_scale_raw[:].bitcast(I32), 0)
-        nc.vector.memset(z_scale[:].bitcast(I32), 0)
-        nc.vector.memset(one[:], 1.0)
-
         table_out = sb.tile([P, 2], F32)
-        nc.scalar.activation(out=table_out[:, 0:1], in_=one[:], func=ACT.Ln)
 
         ident_bf = sb.tile([P, P], BF16)
         ident_f32 = sb.tile([P, P], F32)
-        make_identity(nc, ident_bf[:])
-        make_identity(nc, ident_f32[:])
 
         a_raw = {}
         z_codes = sb.tile([P, PASSES, 2 * J], U8, align_bytes=64)
@@ -87,9 +79,9 @@ def tile_gaussian_mixture_skill_regression_s12_kernel(
             columns = a_words[:, :, 2 * K_PASS * cp : 2 * K_PASS * (cp + 1)]
             nc.sync.dma_start(out=a_raw[cp][:].bitcast(I32), in_=columns.rearrange("g p n -> p g n").bitcast(I32))
 
-        def load_scales(plane, rows):
-            for quad in range(4):
-                nc.sync.dma_start(
+        def load_scales(plane, rows, quads=range(4), queue=nc.sync):
+            for quad in quads:
+                queue.dma_start(
                     out=plane[32 * quad : 32 * quad + 4, :, :].bitcast(I32),
                     in_=rows[:, 4 * quad : 4 * quad + 4, :].rearrange("g r n -> r g n").bitcast(I32),
                 )
@@ -119,48 +111,69 @@ def tile_gaussian_mixture_skill_regression_s12_kernel(
             for i in range(count):
                 x_rows[first + i] = rows[:, i, :]
 
-        for row0, vec in ((0, prior), (PACK, offset)):
-            nc.sync.dma_start(
-                out=vec_rows[row0 : row0 + PACK, :].rearrange("t (b r) -> t b r", r=RUN),
-                in_=vec.rearrange("(b t r) -> t b r", t=PACK, r=RUN),
-            )
+        def load_vectors():
+            for row0, vec in ((0, prior), (PACK, offset)):
+                nc.sync.dma_start(
+                    out=vec_rows[row0 : row0 + PACK, :].rearrange("t (b r) -> t b r", r=RUN),
+                    in_=vec.rearrange("(b t r) -> t b r", t=PACK, r=RUN),
+                )
+
+        def load_z():
+            nc.sync.dma_start(out=z_codes[:].bitcast(I32), in_=z_words.rearrange("g p n -> p g n").bitcast(I32))
+
+        nc.gpsimd.memset(vec_rows[:].bitcast(I32), 0)
+        nc.vector.memset(a_scale_raw[:].bitcast(I32), 0)
+        nc.vector.memset(one[:], 1.0)
+        nc.vector.memset(z_scale[:].bitcast(I32), 0)
+        nc.scalar.activation(out=table_out[:, 0:1], in_=one[:], func=ACT.Ln)
+        make_identity(nc, ident_bf[:])
+        make_identity(nc, ident_f32[:])
+        load_vectors()
         load_scales(a_scale_raw, a_scales)
-        load_a(0)
-        nc.sync.dma_start(out=z_codes[:].bitcast(I32), in_=z_words.rearrange("g p n -> p g n").bitcast(I32))
-        load_scales(z_scale, z_scales)
-        load_a(1)
-        load_mu(0, 0)
         load_x(0, 2)
-        load_x(2, 2)
+        load_mu(0, 0)
+        load_scales(z_scale, z_scales)
+        load_a(0)
+        load_z()
+        load_a(1)
         load_mu(1, 0)
+        load_x(2, 2)
         load_mu(0, 1)
+        load_x(4, 2)
         load_mu(1, 1)
-        for a in range(4, T // P, 2):
+        load_x(6, 2)
+        for a in range(8, T // P, 2):
             load_x(a, 2)
 
-        vecs = sb.tile([P, PASSES, 2 * PACK], F32)
-        pri = vecs[:, :, 0:PACK]
-        off = vecs[:, :, PACK : 2 * PACK]
-        sign01 = sb.tile([P, PASSES, PACK], F32)
         sign = sb.tile([P, PASSES, PACK], F32)
         mag = sb.tile([P, PASSES, PACK], F32)
         below = sb.tile([P, PASSES, PACK], F32)
         above = sb.tile([P, PASSES, PACK], F32)
         factors = sb.tile([P, 2, PASSES, PACK], F32)
         signed_off = sb.tile([P, PASSES, PACK], F32)
+        vec_banks = []
 
         def spread_vectors():
             vec_bank = next_bank([P, PASSES, P], BF16)
             for cp in range(PASSES):
                 nc.tensor.transpose(vec_bank[:, cp, :], vec_rows[:, cp * P : (cp + 1) * P], ident_bf[:])
-            nc.vector.tensor_copy(out=vecs[:], in_=vec_bank[:, :, 0 : 2 * PACK])
-            nc.vector.tensor_scalar(out=sign01[:], in0=pri, scalar1=0.0, scalar2=2.0, op0=ALU.is_ge, op1=ALU.mult)
-            nc.vector.scalar_tensor_tensor(out=mag[:], in0=pri, scalar=-1.0, in1=pri, op0=ALU.mult, op1=ALU.max)
-            nc.vector.tensor_scalar(out=sign[:], in0=sign01[:], scalar1=-1.0, scalar2=None, op0=ALU.add)
-            nc.vector.tensor_scalar(out=below[:], in0=mag[:], scalar1=LN_LOW, scalar2=LN_HIGH, op0=ALU.min, op1=ALU.mult)
-            nc.vector.tensor_scalar(out=above[:], in0=mag[:], scalar1=LN_HIGH, scalar2=LN_LOW, op0=ALU.max, op1=ALU.mult)
-            nc.vector.tensor_scalar(out=factors[:, 0], in0=mag[:], scalar1=LN_LOW, scalar2=LN_HIGH, op0=ALU.max, op1=ALU.min)
-            nc.vector.tensor_tensor(out=signed_off[:], in0=off, in1=sign[:], op=ALU.mult)
+            nc.scalar.activation(out=mag[:], in_=vec_bank[:, :, 0:PACK], func=ACT.Abs)
+            nc.scalar.activation(out=sign[:], in_=vec_bank[:, :, 0:PACK], func=ACT.Sign)
+            vec_banks.append(vec_bank)
+
+        def split_prior():
+            nc.vector.tensor_scalar(
+                out=below[:], in0=mag[:], scalar1=LN_LOW, scalar2=LN_HIGH, op0=ALU.min, op1=ALU.mult
+            )
+            nc.vector.tensor_scalar(
+                out=above[:], in0=mag[:], scalar1=LN_HIGH, scalar2=LN_LOW, op0=ALU.max, op1=ALU.mult
+            )
+            nc.vector.tensor_scalar(
+                out=factors[:, 0], in0=mag[:], scalar1=LN_LOW, scalar2=LN_HIGH, op0=ALU.max, op1=ALU.min
+            )
+            nc.vector.tensor_tensor(
+                out=signed_off[:], in0=vec_banks[0][:, :, PACK : 2 * PACK], in1=sign[:], op=ALU.mult
+            )
             nc.vector.scalar_tensor_tensor(
                 out=factors[:, 1], in0=below[:], scalar=LN_LOW, in1=above[:], op0=ALU.max, op1=ALU.mult
             )
@@ -192,21 +205,22 @@ def tile_gaussian_mixture_skill_regression_s12_kernel(
         x_grouped = {}
         x_q = {}
         h_slots = {}
+        h_grouped = {}
         h_q = {}
         out_banks = {}
 
         def interleave_mu(kp, cp):
-            grouped = sb.tile([P, PACK, P, PACK], BF16, name="mu_grouped", tag="mu_grouped", bufs=2, align_bytes=64)
-            src = mu_raw[kp, cp][:].rearrange("p j (q t h i) -> p t q h j i", t=PACK, h=2, i=4)
-            dst = grouped[:].rearrange("p t (q h i) j -> p t q h j i", h=2, i=4)
-            for t in range(PACK):
-                nc.vector.tensor_copy(out=dst[:, t], in_=src[:, t])
+            grouped = sb.tile([P, PACK, P, PACK], BF16, name="mu_grouped", tag="mu_grouped", bufs=3, align_bytes=64)
+            src = mu_raw[kp, cp][:].rearrange("p j (q t h i) -> p h t q j i", t=PACK, h=2, i=4)
+            dst = grouped[:].rearrange("p t (q h i) j -> p h t q j i", h=2, i=4)
+            for h in range(2):
+                nc.vector.tensor_copy(out=dst[:, h], in_=src[:, h])
             mu_grouped[kp, cp] = grouped[:].rearrange("p t m j -> p (t m j)")
 
         def quantize_mu(kp, cp):
             mu_q[kp, cp] = quantize(mu_grouped[kp, cp], K_PASS, "mu", 4)
 
-        def local_models(cp, t):
+        def local_models(cp, t, on_scalar=True):
             if t == 0:
                 l_slots[cp] = sb.tile([P, PACK, J], BF16, name="l_slots", tag="l_slots", bufs=2)
             bank = next_bank([P, J], F32)
@@ -221,13 +235,15 @@ def tile_gaussian_mixture_skill_regression_s12_kernel(
                     start=(kp == 0),
                     stop=(kp == PASSES - 1),
                 )
-            nc.scalar.activation(
-                out=l_slots[cp][:, t, :],
-                in_=bank[:],
-                func=ACT.Identity,
-                scale=sign[:, cp, t : t + 1],
-                bias=signed_off[:, cp, t : t + 1],
-            )
+            factor, shift = sign[:, cp, t : t + 1], signed_off[:, cp, t : t + 1]
+            if on_scalar:
+                nc.scalar.activation(
+                    out=l_slots[cp][:, t, :], in_=bank[:], func=ACT.Identity, scale=factor, bias=shift
+                )
+            else:
+                nc.vector.tensor_scalar(
+                    out=l_slots[cp][:, t, :], in0=bank[:], scalar1=factor, scalar2=shift, op0=ALU.mult, op1=ALU.add
+                )
 
         def interleave_l(cp):
             l_grouped[cp] = interleave(l_slots[cp][:], J, "l_grouped", 2)
@@ -267,25 +283,33 @@ def tile_gaussian_mixture_skill_regression_s12_kernel(
                 move(out=x_grouped[g][:, :, i * P : (i + 1) * P, :], in_=bank[:].rearrange("p g u r -> p g r u"))
 
         def quantize_x(g):
+            grouped = x_grouped[g][:].rearrange("p g n u -> p (g n u)").bitcast(BF16)
+            codes, scales = quantize(grouped, PASSES * GROUP, "x", 2)
             for kp in range(PASSES):
-                grouped = x_grouped[g][:, kp].rearrange("p n u -> p (n u)").bitcast(BF16)
-                x_q[g, kp] = quantize(grouped, GROUP, "x", 4)
+                cols = slice(kp * GROUP, (kp + 1) * GROUP)
+                x_q[g, kp, 0] = (codes[:, cols], scales[:, cols])
 
-        def responsibilities(g, cp, col0=0, width=GROUP):
-            if col0 == 0:
+        def quantize_x_half(g, col0):
+            for kp in range(PASSES):
+                grouped = x_grouped[g][:, kp, col0 : col0 + HALF].rearrange("p n u -> p (n u)").bitcast(BF16)
+                codes, scales = quantize(grouped, HALF, "xh", 4)
+                x_q[g, kp, col0] = (codes[:], scales[:])
+
+        def responsibilities(g, cp, col0=0, width=GROUP, slots=range(PACK)):
+            if (g, cp) not in h_slots:
                 h_slots[g, cp] = sb.tile([P, PACK, GROUP], BF16, name="h_slots", tag="h_slots", bufs=5)
             cols = slice(col0, col0 + width)
-            for t in range(PACK):
+            for t in slots:
                 bank = next_bank([P, width], F32)
                 for kp in range(PASSES):
                     w_codes, w_scales = mu_q[kp, cp]
-                    x_codes, x_scales = x_q[g, kp]
+                    x_codes, x_scales = x_q[g, kp, col0]
                     nc.tensor.matmul_mx(
                         out=bank[:],
                         lhsT=w_codes[:, t * P : (t + 1) * P].bitcast(FP8X4),
                         lhsT_scale=w_scales[:, t * P : (t + 1) * P],
-                        rhs=x_codes[:, cols].bitcast(FP8X4),
-                        rhs_scale=x_scales[:, cols],
+                        rhs=x_codes.bitcast(FP8X4),
+                        rhs_scale=x_scales,
                         start=(kp == 0),
                         stop=(kp == PASSES - 1),
                     )
@@ -293,18 +317,15 @@ def tile_gaussian_mixture_skill_regression_s12_kernel(
                     out=h_slots[g, cp][:, t, cols], in_=bank[:], func=ACT.Exp, bias=log_prior[:, cp, t : t + 1]
                 )
 
-        def quantize_h(g, cp, width, col0=0, count=2):
-            tag = "h%d" % width
-            grouped = []
-            for i in range(count + 1):
-                if i < count:
-                    slots = h_slots[g, cp][:, :, col0 + i * width : col0 + (i + 1) * width]
-                    grouped.append(interleave(slots, width, tag + "_grouped", 4))
-                if i > 0:
-                    codes, scales = quantize(grouped[i - 1], width, tag, 10)
-                    first = g * TILES_PER_GROUP + (col0 + (i - 1) * width) // P
-                    for j in range(width // P):
-                        h_q[first + j, cp] = (codes[:, j * P : (j + 1) * P], scales[:, j * P : (j + 1) * P])
+        def interleave_h(g, cp, col0=0, width=GROUP):
+            slots = h_slots[g, cp][:, :, col0 : col0 + width]
+            h_grouped[g, cp, col0] = interleave(slots, width, "h_grouped", 3)
+
+        def quantize_h(g, cp, col0=0, width=GROUP):
+            codes, scales = quantize(h_grouped[g, cp, col0], width, "h", 8)
+            first = g * TILES_PER_GROUP + col0 // P
+            for j in range(width // P):
+                h_q[first + j, cp] = (codes[:, j * P : (j + 1) * P], scales[:, j * P : (j + 1) * P])
 
         def blend(a, col0=0, width=J):
             bank = next_bank([P, width], F32)
@@ -331,73 +352,87 @@ def tile_gaussian_mixture_skill_regression_s12_kernel(
             nc.sync.dma_start(out=out[a * P : (a + 1) * P, col0 : col0 + width], in_=result[:])
 
         spread_vectors()
-        sort_a_scales()
-        sort_a(0)
-        sort_a(1)
+        split_prior()
         nc.scalar.activation(out=logs[:], in_=factors[:], func=ACT.Ln)
         nc.scalar.activation(out=table_out[:, 1:2], in_=one[:], func=ACT.Exp)
+        turn_x((0, 1))
+        sort_a_scales()
         interleave_mu(0, 0)
-        nc.vector.tensor_tensor(out=log_prior[:], in0=logs[:, 0], in1=logs[:, 1], op=ALU.add)
+        sort_a(0)
         quantize_mu(0, 0)
+        nc.vector.tensor_tensor(out=log_prior[:], in0=logs[:, 0], in1=logs[:, 1], op=ALU.add)
+        sort_a(1)
+        interleave_mu(1, 0)
+
+        quantize_mu(1, 0)
         for t in range(PACK):
             local_models(0, t)
-        turn_x(range(0, 4))
-        interleave_mu(1, 0)
-        quantize_mu(1, 0)
+        interleave_mu(0, 1)
+        turn_x((2, 3), ())
+
         for t in range(PACK):
             local_models(1, t)
         quantize_x(0)
-        interleave_mu(0, 1)
-        interleave_mu(1, 1)
         quantize_mu(0, 1)
+        turn_x((4, 5))
+        interleave_mu(1, 1)
+        interleave_l(0)
         quantize_mu(1, 1)
 
         responsibilities(0, 0)
-        interleave_l(0)
-        turn_x(range(4, 8), ())
-        quantize_x(1)
-        responsibilities(0, 1)
-
-        responsibilities(1, 0)
         interleave_l(1)
         quantize_l(0)
+        turn_x((6, 7))
+        quantize_x(1)
+        responsibilities(0, 1)
+        sort_x(8)
+        sort_x(10)
         quantize_l(1)
+        interleave_h(0, 0)
 
-        turn_x(range(8, 12), ())
-        quantize_h(0, 0, HALF)
-        quantize_h(0, 1, HALF)
-        responsibilities(1, 1)
+        responsibilities(1, 0)
+        interleave_h(0, 1)
+        quantize_h(0, 0)
+        quantize_h(0, 1)
+        turn_x(range(8, 12), (11,))
         quantize_x(2)
+        interleave_h(1, 0)
+        responsibilities(1, 1)
         for a in range(0, 4):
             blend(a)
-            store(a, a not in (7, 13))
-
+            store(a, a not in (3, 6, 7, 13))
         sort_x(12)
         sort_x(14)
+
         responsibilities(2, 0)
-        quantize_h(1, 0, HALF)
-        quantize_h(1, 1, HALF)
-        turn_x(range(12, 16), (14, 15))
-        responsibilities(2, 1)
+        interleave_h(1, 1)
+        quantize_h(1, 0)
+        quantize_h(1, 1)
+        turn_x(range(12, 16), (15,))
+        interleave_h(2, 0)
         quantize_x(3)
-        quantize_h(2, 0, HALF)
+        responsibilities(2, 1)
+        interleave_h(2, 1)
+        quantize_h(2, 0)
+        quantize_h(2, 1)
         for a in range(4, 8):
             blend(a)
-        for a in range(4, 8):
-            if a not in (7, 13):
-                store(a, True)
-        quantize_h(2, 1, HALF)
-        for a in range(4, 8):
-            if a in (7, 13):
-                store(a, False)
+            store(a, a not in (3, 6, 7, 13))
 
         responsibilities(3, 0)
-        quantize_h(3, 0, HALF)
+        blend(8)
+        interleave_h(3, 0)
+        store(8, False)
         responsibilities(3, 1)
-        quantize_h(3, 1, P, 0, 4)
-        for a in range(8, 15):
+        quantize_h(3, 0)
+        for i in range(TILES_PER_GROUP + 1):
+            if i < TILES_PER_GROUP:
+                interleave_h(3, 1, i * P, P)
+            if i > 0:
+                quantize_h(3, 1, (i - 1) * P, P)
+        for a in range(9, 15):
             blend(a)
-            store(a, a not in (7, 13))
+            store(a, a not in (3, 6, 7, 13))
         for half in range(2):
             blend(15, half * HALF, HALF)
             store(15, half == 1, half * HALF, HALF)

@@ -385,30 +385,31 @@ def tile_gaussian_mixture_skill_regression_s12_kernel(
         turn_x((6, 7))
         quantize_x(1)
         responsibilities(0, 1)
-        sort_x(8)
-        sort_x(10)
         quantize_l(1)
         interleave_h(0, 0)
+        turn_x((8, 9), ())
 
         responsibilities(1, 0)
         interleave_h(0, 1)
         quantize_h(0, 0)
         quantize_h(0, 1)
-        turn_x(range(8, 12), (11,))
-        quantize_x(2)
+        turn_x((10, 11), ())
         interleave_h(1, 0)
+        quantize_x(2)
         responsibilities(1, 1)
-        for a in range(0, 4):
+        for a in range(0, 2):
             blend(a)
-            store(a, a not in (3, 6, 7, 13))
-        sort_x(12)
-        sort_x(14)
+            store(a, a not in (0, 1, 2, 3, 6, 7, 13))
+        turn_x((12, 13), ())
+        for a in range(2, 4):
+            blend(a)
+            store(a, a not in (0, 1, 2, 3, 6, 7, 13))
 
         responsibilities(2, 0)
         interleave_h(1, 1)
         quantize_h(1, 0)
         quantize_h(1, 1)
-        turn_x(range(12, 16), (15,))
+        turn_x((14, 15), ())
         interleave_h(2, 0)
         quantize_x(3)
         responsibilities(2, 1)
@@ -417,7 +418,7 @@ def tile_gaussian_mixture_skill_regression_s12_kernel(
         quantize_h(2, 1)
         for a in range(4, 8):
             blend(a)
-            store(a, a not in (3, 6, 7, 13))
+            store(a, a not in (0, 1, 2, 3, 6, 7, 13))
 
         responsibilities(3, 0)
         blend(8)
@@ -432,7 +433,7 @@ def tile_gaussian_mixture_skill_regression_s12_kernel(
                 quantize_h(3, 1, (i - 1) * P, P)
         for a in range(9, 15):
             blend(a)
-            store(a, a not in (3, 6, 7, 13))
+            store(a, a not in (0, 1, 2, 3, 6, 7, 13))
         for half in range(2):
             blend(15, half * HALF, HALF)
             store(15, half == 1, half * HALF, HALF)

from contextlib import ExitStack

import concourse.mybir as mybir
from concourse.masks import make_identity

T, F, C, D, J = 2048, 1024, 1024, 1024, 512
FLOPS = 2 * (T * F * C + D * C * J + T * C * J)

F32 = mybir.dt.float32
BF16 = mybir.dt.bfloat16
I32 = mybir.dt.int32
U32 = mybir.dt.uint32
U8 = mybir.dt.uint8
FP8X4 = mybir.dt.float8_e4m3fn_x4
FP4X4 = mybir.dt.float4_e2m1fn_x4
ACT = mybir.ActivationFunctionType
ALU = mybir.AluOpType

P = 128
PACK = 4
K_PASS = P * PACK
PASSES = 2
GROUP = 512
HALF = GROUP // 2
TILES_PER_GROUP = GROUP // P
GROUPS = T // GROUP
BANKS = 8
RUN = 8
LN_LOW = 2.0 ** -63
LN_HIGH = 2.0 ** 63


def tile_gaussian_mixture_skill_regression_s12_kernel(
    tc, x, mu, prior, a_words, a_scales, z_words, z_scales, offset, out
):
    nc = tc.nc

    with ExitStack() as ctx:
        sb = ctx.enter_context(tc.tile_pool(name="sb", bufs=1))
        psum = ctx.enter_context(tc.psum_pool(name="psum", bufs=1))
        ctx.enter_context(tc.manual_schedule())

        banks_taken = []

        def next_bank(shape, dtype):
            tag = "bank%d" % (len(banks_taken) % BANKS)
            banks_taken.append(tag)
            bank = psum.tile(shape, dtype, name=tag, tag=tag)
            return bank

        def quantize(grouped, width, tag, bufs):
            codes = sb.tile([P, width], U32, name=tag + "_codes", tag=tag + "_codes", bufs=bufs, align_bytes=64)
            scales = sb.tile([P, width], U8, name=tag + "_scales", tag=tag + "_scales", bufs=bufs, align_bytes=64)
            nc.vector.quantize_mx(out=codes[:].bitcast(FP8X4), scales=scales[:], in_=grouped)
            return codes, scales

        def interleave(slots, width, tag, bufs):
            grouped = sb.tile([P, width, PACK], BF16, name=tag, tag=tag, bufs=bufs, align_bytes=64)
            nc.vector.tensor_copy(
                out=grouped[:].rearrange("p (c i) t -> p c t i", i=4),
                in_=slots.rearrange("p t (c i) -> p c t i", i=4),
            )
            return grouped[:].rearrange("p n t -> p (n t)")

        a_scale_raw = sb.tile([P, PASSES, C], U8, align_bytes=64)
        z_scale = sb.tile([P, PASSES, J], U8, align_bytes=64)
        vec_rows = sb.tile([P, 2 * P], BF16)
        one = sb.tile([P, 1], F32)
        table_out = sb.tile([P, 2], F32)

        ident_bf = sb.tile([P, P], BF16)
        ident_f32 = sb.tile([P, P], F32)

        a_raw = {}
        z_codes = sb.tile([P, PASSES, 2 * J], U8, align_bytes=64)

        def load_a(cp):
            a_raw[cp] = sb.tile([P, PASSES, 2 * K_PASS], U8, name="a_raw", tag="a_raw", bufs=2)
            columns = a_words[:, :, 2 * K_PASS * cp : 2 * K_PASS * (cp + 1)]
            nc.sync.dma_start(out=a_raw[cp][:].bitcast(I32), in_=columns.rearrange("g p n -> p g n").bitcast(I32))

        def load_scales(plane, rows, quads=range(4), queue=nc.sync):
            for quad in quads:
                queue.dma_start(
                    out=plane[32 * quad : 32 * quad + 4, :, :].bitcast(I32),
                    in_=rows[:, 4 * quad : 4 * quad + 4, :].rearrange("g r n -> r g n").bitcast(I32),
                )

        mu_raw = {}
        x_rows = {}
        x_pairs = {}
        x_sorted = {}

        def load_mu(kp, cp):
            raw = sb.tile([P, PACK, K_PASS], BF16, name="mu_raw", tag="mu_raw", bufs=4)
            nc.sync.dma_start(
                out=raw[:],
                in_=mu[kp * K_PASS : (kp + 1) * K_PASS, cp * K_PASS : (cp + 1) * K_PASS].rearrange(
                    "(p j) c -> p j c", j=PACK
                ),
            )
            mu_raw[kp, cp] = raw

        def load_x(first, count):
            tag = "x_rows%d" % first
            rows = sb.tile([P, count, F], BF16, name=tag, tag=tag)
            nc.sync.dma_start(
                out=rows[:], in_=x[first * P : (first + count) * P, :].rearrange("(a p) k -> p a k", p=P)
            )
            x_pairs[first] = rows
            for i in range(count):
                x_rows[first + i] = rows[:, i, :]

        def load_vectors():
            for row0, vec in ((0, prior), (PACK, offset)):
                nc.sync.dma_start(
                    out=vec_rows[row0 : row0 + PACK, :].rearrange("t (b r) -> t b r", r=RUN),
                    in_=vec.rearrange("(b t r) -> t b r", t=PACK, r=RUN),
                )

        def load_z():
            nc.sync.dma_start(out=z_codes[:].bitcast(I32), in_=z_words.rearrange("g p n -> p g n").bitcast(I32))

        nc.gpsimd.memset(vec_rows[:].bitcast(I32), 0)
        nc.vector.memset(a_scale_raw[:].bitcast(I32), 0)
        nc.vector.memset(one[:], 1.0)
        nc.vector.memset(z_scale[:].bitcast(I32), 0)
        nc.scalar.activation(out=table_out[:, 0:1], in_=one[:], func=ACT.Ln)
        make_identity(nc, ident_bf[:])
        make_identity(nc, ident_f32[:])
        load_vectors()
        load_scales(a_scale_raw, a_scales)
        load_x(0, 2)
        load_mu(0, 0)
        load_scales(z_scale, z_scales)
        load_a(0)
        load_z()
        load_a(1)
        load_mu(1, 0)
        load_x(2, 2)
        load_mu(0, 1)
        load_x(4, 2)
        load_mu(1, 1)
        load_x(6, 2)
        for a in range(8, T // P, 2):
            load_x(a, 2)

        sign = sb.tile([P, PASSES, PACK], F32)
        mag = sb.tile([P, PASSES, PACK], F32)
        below = sb.tile([P, PASSES, PACK], F32)
        above = sb.tile([P, PASSES, PACK], F32)
        factors = sb.tile([P, 2, PASSES, PACK], F32)
        signed_off = sb.tile([P, PASSES, PACK], F32)
        vec_banks = []

        def spread_vectors():
            vec_bank = next_bank([P, PASSES, P], BF16)
            for cp in range(PASSES):
                nc.tensor.transpose(vec_bank[:, cp, :], vec_rows[:, cp * P : (cp + 1) * P], ident_bf[:])
            nc.scalar.activation(out=mag[:], in_=vec_bank[:, :, 0:PACK], func=ACT.Abs)
            nc.scalar.activation(out=sign[:], in_=vec_bank[:, :, 0:PACK], func=ACT.Sign)
            vec_banks.append(vec_bank)

        def split_prior():
            nc.vector.tensor_scalar(
                out=below[:], in0=mag[:], scalar1=LN_LOW, scalar2=LN_HIGH, op0=ALU.min, op1=ALU.mult
            )
            nc.vector.tensor_scalar(
                out=above[:], in0=mag[:], scalar1=LN_HIGH, scalar2=LN_LOW, op0=ALU.max, op1=ALU.mult
            )
            nc.vector.tensor_scalar(
                out=factors[:, 0], in0=mag[:], scalar1=LN_LOW, scalar2=LN_HIGH, op0=ALU.max, op1=ALU.min
            )
            nc.vector.tensor_tensor(
                out=signed_off[:], in0=vec_banks[0][:, :, PACK : 2 * PACK], in1=sign[:], op=ALU.mult
            )
            nc.vector.scalar_tensor_tensor(
                out=factors[:, 1], in0=below[:], scalar=LN_LOW, in1=above[:], op0=ALU.max, op1=ALU.mult
            )

        logs = sb.tile([P, 2, PASSES, PACK], F32)
        log_prior = sb.tile([P, PASSES, PACK], F32)

        a_scale = sb.tile([P, PASSES, C], U8, align_bytes=64)
        a_codes = {}

        def sort_a_scales():
            nc.vector.tensor_copy(
                out=a_scale[:].bitcast(I32).rearrange("p g (h t q w) -> p (g h) t q w", h=PASSES, t=PACK, w=2),
                in_=a_scale_raw[:].bitcast(I32).rearrange("p g (h q t w) -> p (g h) t q w", h=PASSES, t=PACK, w=2),
            )

        def sort_a(cp):
            a_codes[cp] = sb.tile([P, PASSES, 2 * K_PASS], U8, name="a_codes", tag="a_codes", bufs=2, align_bytes=64)
            nc.vector.tensor_copy(
                out=a_codes[cp][:].bitcast(I32).rearrange("p g (t q w) -> p g t q w", t=PACK, w=4),
                in_=a_raw[cp][:].bitcast(I32).rearrange("p g (q t w) -> p g t q w", t=PACK, w=4),
            )

        mu_grouped = {}
        mu_q = {}
        l_slots = {}
        l_grouped = {}
        l_q = {}
        x_grouped = {}
        x_q = {}
        h_slots = {}
        h_grouped = {}
        h_q = {}
        out_banks = {}

        def interleave_mu(kp, cp):
            grouped = sb.tile([P, PACK, P, PACK], BF16, name="mu_grouped", tag="mu_grouped", bufs=3, align_bytes=64)
            src = mu_raw[kp, cp][:].rearrange("p j (q t h i) -> p h t q j i", t=PACK, h=2, i=4)
            dst = grouped[:].rearrange("p t (q h i) j -> p h t q j i", h=2, i=4)
            for h in range(2):
                nc.vector.tensor_copy(out=dst[:, h], in_=src[:, h])
            mu_grouped[kp, cp] = grouped[:].rearrange("p t m j -> p (t m j)")

        def quantize_mu(kp, cp):
            mu_q[kp, cp] = quantize(mu_grouped[kp, cp], K_PASS, "mu", 4)

        def local_models(cp, t, on_scalar=True):
            if t == 0:
                l_slots[cp] = sb.tile([P, PACK, J], BF16, name="l_slots", tag="l_slots", bufs=2)
            bank = next_bank([P, J], F32)
            col = (cp * PACK + t) * P
            for kp in range(PASSES):
                nc.tensor.matmul_mx(
                    out=bank[:],
                    lhsT=a_codes[cp][:, kp, 2 * t * P : 2 * (t + 1) * P].bitcast(FP4X4),
                    lhsT_scale=a_scale[:, kp, col : col + P],
                    rhs=z_codes[:, kp, :].bitcast(FP4X4),
                    rhs_scale=z_scale[:, kp, :],
                    start=(kp == 0),
                    stop=(kp == PASSES - 1),
                )
            factor, shift = sign[:, cp, t : t + 1], signed_off[:, cp, t : t + 1]
            if on_scalar:
                nc.scalar.activation(
                    out=l_slots[cp][:, t, :], in_=bank[:], func=ACT.Identity, scale=factor, bias=shift
                )
            else:
                nc.vector.tensor_scalar(
                    out=l_slots[cp][:, t, :], in0=bank[:], scalar1=factor, scalar2=shift, op0=ALU.mult, op1=ALU.add
                )

        def interleave_l(cp):
            l_grouped[cp] = interleave(l_slots[cp][:], J, "l_grouped", 2)

        def quantize_l(cp):
            l_q[cp] = quantize(l_grouped[cp], J, "l", 2)

        def sort_x(first):
            ordered = sb.tile([P, 2, PASSES, 2, P], F32, name="x_sorted", tag="x_sorted", bufs=2)
            nc.vector.tensor_copy(
                out=ordered[:].rearrange("p a g u (c i) -> p (a g) c u i", i=4),
                in_=x_pairs[first][:].bitcast(F32).rearrange("p a (g c i u) -> p (a g) c u i", g=PASSES, i=4, u=2),
            )
            for i in range(2):
                x_sorted[first + i] = ordered[:, i]

        def turn_x(tiles, on_vector=()):
            turned = []
            for a in tiles:
                bank = next_bank([P, PASSES, 2, P], F32)
                words = x_rows[a].bitcast(F32)
                for kp in range(PASSES):
                    for u in range(2):
                        if a in x_sorted:
                            source = x_sorted[a][:, kp, u, :]
                        else:
                            source = words[:, 256 * kp + u : 256 * (kp + 1) : 2]
                        nc.tensor.transpose(bank[:, kp, u, :], source, ident_f32[:])
                turned.append((a, bank))
            for a, bank in turned:
                g, i = divmod(a, TILES_PER_GROUP)
                if i == 0:
                    x_grouped[g] = sb.tile(
                        [P, PASSES, GROUP, 2], F32, name="x_grouped", tag="x_grouped", bufs=2, align_bytes=64
                    )
                move = nc.vector.tensor_copy if a in on_vector else nc.scalar.copy
                move(out=x_grouped[g][:, :, i * P : (i + 1) * P, :], in_=bank[:].rearrange("p g u r -> p g r u"))

        def quantize_x(g):
            grouped = x_grouped[g][:].rearrange("p g n u -> p (g n u)").bitcast(BF16)
            codes, scales = quantize(grouped, PASSES * GROUP, "x", 2)
            for kp in range(PASSES):
                cols = slice(kp * GROUP, (kp + 1) * GROUP)
                x_q[g, kp, 0] = (codes[:, cols], scales[:, cols])

        def quantize_x_half(g, col0):
            for kp in range(PASSES):
                grouped = x_grouped[g][:, kp, col0 : col0 + HALF].rearrange("p n u -> p (n u)").bitcast(BF16)
                codes, scales = quantize(grouped, HALF, "xh", 4)
                x_q[g, kp, col0] = (codes[:], scales[:])

        def responsibilities(g, cp, col0=0, width=GROUP, slots=range(PACK)):
            if (g, cp) not in h_slots:
                h_slots[g, cp] = sb.tile([P, PACK, GROUP], BF16, name="h_slots", tag="h_slots", bufs=5)
            cols = slice(col0, col0 + width)
            for t in slots:
                bank = next_bank([P, width], F32)
                for kp in range(PASSES):
                    w_codes, w_scales = mu_q[kp, cp]
                    x_codes, x_scales = x_q[g, kp, col0]
                    nc.tensor.matmul_mx(
                        out=bank[:],
                        lhsT=w_codes[:, t * P : (t + 1) * P].bitcast(FP8X4),
                        lhsT_scale=w_scales[:, t * P : (t + 1) * P],
                        rhs=x_codes.bitcast(FP8X4),
                        rhs_scale=x_scales,
                        start=(kp == 0),
                        stop=(kp == PASSES - 1),
                    )
                nc.scalar.activation(
                    out=h_slots[g, cp][:, t, cols], in_=bank[:], func=ACT.Exp, bias=log_prior[:, cp, t : t + 1]
                )

        def interleave_h(g, cp, col0=0, width=GROUP):
            slots = h_slots[g, cp][:, :, col0 : col0 + width]
            h_grouped[g, cp, col0] = interleave(slots, width, "h_grouped", 3)

        def quantize_h(g, cp, col0=0, width=GROUP):
            codes, scales = quantize(h_grouped[g, cp, col0], width, "h", 8)
            first = g * TILES_PER_GROUP + col0 // P
            for j in range(width // P):
                h_q[first + j, cp] = (codes[:, j * P : (j + 1) * P], scales[:, j * P : (j + 1) * P])

        def blend(a, col0=0, width=J):
            bank = next_bank([P, width], F32)
            for cp in range(PASSES):
                h_codes, h_scales = h_q[a, cp]
                l_codes, l_scales = l_q[cp]
                nc.tensor.matmul_mx(
                    out=bank[:],
                    lhsT=h_codes.bitcast(FP8X4),
                    lhsT_scale=h_scales,
                    rhs=l_codes[:, col0 : col0 + width].bitcast(FP8X4),
                    rhs_scale=l_scales[:, col0 : col0 + width],
                    start=(cp == 0),
                    stop=(cp == PASSES - 1),
                )
            out_banks[a, col0] = bank

        def store(a, on_scalar, col0=0, width=J):
            result = sb.tile([P, width], F32, name="result", tag="result", bufs=8)
            if on_scalar:
                nc.scalar.copy(out=result[:], in_=out_banks[a, col0][:])
            else:
                nc.vector.tensor_copy(out=result[:], in_=out_banks[a, col0][:])
            nc.sync.dma_start(out=out[a * P : (a + 1) * P, col0 : col0 + width], in_=result[:])

        spread_vectors()
        split_prior()
        nc.scalar.activation(out=logs[:], in_=factors[:], func=ACT.Ln)
        nc.scalar.activation(out=table_out[:, 1:2], in_=one[:], func=ACT.Exp)
        turn_x((0, 1))
        sort_a_scales()
        interleave_mu(0, 0)
        sort_a(0)
        quantize_mu(0, 0)
        nc.vector.tensor_tensor(out=log_prior[:], in0=logs[:, 0], in1=logs[:, 1], op=ALU.add)
        sort_a(1)
        interleave_mu(1, 0)

        quantize_mu(1, 0)
        for t in range(PACK):
            local_models(0, t)
        interleave_mu(0, 1)
        turn_x((2, 3), ())

        for t in range(PACK):
            local_models(1, t)
        quantize_x(0)
        quantize_mu(0, 1)
        turn_x((4, 5))
        interleave_mu(1, 1)
        interleave_l(0)
        quantize_mu(1, 1)

        responsibilities(0, 0)
        interleave_l(1)
        quantize_l(0)
        turn_x((6, 7))
        quantize_x(1)
        responsibilities(0, 1)
        quantize_l(1)
        interleave_h(0, 0)
        turn_x((8, 9), ())

        responsibilities(1, 0)
        interleave_h(0, 1)
        quantize_h(0, 0)
        quantize_h(0, 1)
        turn_x((10, 11), ())
        interleave_h(1, 0)
        quantize_x(2)
        responsibilities(1, 1)
        for a in range(0, 2):
            blend(a)
            store(a, a not in (0, 1, 2, 3, 6, 7, 13))
        turn_x((12, 13), ())
        for a in range(2, 4):
            blend(a)
            store(a, a not in (0, 1, 2, 3, 6, 7, 13))

        responsibilities(2, 0)
        interleave_h(1, 1)
        quantize_h(1, 0)
        quantize_h(1, 1)
        turn_x((14, 15), ())
        interleave_h(2, 0)
        quantize_x(3)
        responsibilities(2, 1)
        interleave_h(2, 1)
        quantize_h(2, 0)
        quantize_h(2, 1)
        for a in range(4, 8):
            blend(a)
            store(a, a not in (0, 1, 2, 3, 6, 7, 13))

        responsibilities(3, 0)
        blend(8)
        interleave_h(3, 0)
        store(8, False)
        responsibilities(3, 1)
        quantize_h(3, 0)
        for i in range(TILES_PER_GROUP + 1):
            if i < TILES_PER_GROUP:
                interleave_h(3, 1, i * P, P)
            if i > 0:
                quantize_h(3, 1, (i - 1) * P, P)
        for a in range(9, 15):
            blend(a)
            store(a, a not in (0, 1, 2, 3, 6, 7, 13))
        for half in range(2):
            blend(15, half * HALF, HALF)
            store(15, half == 1, half * HALF, HALF)
